import numpy as np
import ml_dtypes


def mxq(x, axis, fmt="e4m3"):
    dtype, down = {"e4m3": (ml_dtypes.float8_e4m3fn, 7), "e5m2": (ml_dtypes.float8_e5m2, 14)}[fmt]
    v = np.moveaxis(np.asarray(x, np.float32).astype(ml_dtypes.bfloat16).astype(np.float64), axis, -1)
    blocks = v.reshape(v.shape[:-1] + (-1, 32))
    amax = np.abs(blocks).max(-1, keepdims=True)
    byte = np.maximum(np.where(amax > 0, np.frexp(amax)[1] - 1 + 127, 0) - down, 1)
    scale = np.exp2(byte - 127.0)
    codes = (blocks / scale).astype(np.float32).astype(dtype).astype(np.float64)
    return np.moveaxis((codes * scale).reshape(v.shape), -1, axis)


WIDE = False


def mx_kscale(k):
    if not WIDE:
        return np.ones(k)
    levels = np.array([10, -10, 5, -5, 0])
    if k % 512:
        return np.exp2(np.random.permutation(np.resize(levels, k // 32))).repeat(32)
    a = np.empty((k // 512, 16))
    for p in range(k // 512):
        a[p, :8] = np.random.permutation(np.resize(levels, 8))
        for g in range(8):
            far = levels[np.abs(levels - a[p, g]) >= 10]
            a[p, g + 8] = far[np.random.randint(len(far))]
    return np.exp2(a.ravel()).repeat(32)


def f64(x):
    return np.asarray(x).astype(np.float64)


def striped(idx):
    return np.tile(idx.reshape(-1, 16).T, (8, 1)).astype(np.uint16)


def unstriped(offs):
    return offs[:16].T.reshape(-1).astype(np.int64)


E2M1 = np.array([0.0, 0.5, 1.0, 1.5, 2.0, 3.0, 4.0, 6.0, -0.0, -0.5, -1.0, -1.5, -2.0, -3.0, -4.0, -6.0])


def pack_weight(w, fmt):
    k, n = w.shape
    w = f64(np.asarray(w, np.float32).astype(ml_dtypes.bfloat16)).reshape(k // 32, 32, n)
    amax = np.abs(w).max(1)
    if fmt == "e4m3":
        byte = np.frexp(amax)[1] - 1 + 127 - 7
    else:
        mant, ex = np.frexp(amax / 6.0)
        byte = np.where(mant > 0.5, ex, ex - 1) + 127
    byte = np.clip(np.where(amax > 0, byte, 1), 1, 254)
    scaled = (w * np.exp2(127.0 - byte)[:, None, :]).reshape(k, n).astype(np.float32)
    by_word = np.ascontiguousarray(scaled.reshape(k // 512, 128, 4, n).transpose(0, 1, 3, 2))
    if fmt == "e4m3":
        words = by_word.astype(ml_dtypes.float8_e4m3fn).view(np.uint8)
    else:
        c = by_word.astype(ml_dtypes.float4_e2m1fn).view(np.uint8) & 0xF
        words = (c[..., 0::2] | (c[..., 1::2] << 4)).reshape(k // 512, 128, 2 * n)
    return np.ascontiguousarray(words), np.ascontiguousarray(byte.astype(np.uint8).reshape(k // 512, 16, n))


def unpack_weight(words, scales, fmt):
    g, _, n = scales.shape
    words = np.ascontiguousarray(words).reshape(g, 128, n, -1)
    if fmt == "e4m3":
        vals = words.view(ml_dtypes.float8_e4m3fn).astype(np.float64)
    else:
        nib = np.empty((g, 128, n, 4), np.uint8)
        nib[..., 0::2] = words & 0xF
        nib[..., 1::2] = words >> 4
        vals = E2M1[nib]
    vals = vals * np.repeat(np.exp2(scales.astype(np.float64) - 127.0), 8, axis=1)[..., None]
    return vals.transpose(0, 1, 3, 2).reshape(g * 512, n)


K, T, E, C, N = 1536, 768, 6, 128, 384
TOP = 4
PAD = 64
K8 = 512


def by_expert(wq, xq):
    return np.concatenate([wq[e].T @ xq[:, e * C:(e + 1) * C] for e in range(E)], axis=1)


def setup_inputs():
    n = np.random.standard_normal
    s = mx_kscale(K)[:, None]
    slot_token = np.empty(E * C, np.int64); pos = np.tile(E * C + np.arange(T) % PAD, (TOP, 1)); taken = np.zeros(T, np.int64)
    liked = np.random.randn(T)
    for e in np.random.permutation(E):
        free = np.flatnonzero(taken < TOP); pick = np.random.permutation(free[np.argsort(-(liked[free] + np.random.gumbel(size=free.size)))[:C]]); slot_token[e * C:(e + 1) * C] = pick
        pos[taken[pick], pick] = e * C + np.arange(C); taken[pick] += 1
    g = np.random.uniform(0.2, 0.8, (TOP, T))
    w = n((E, K, N)) / np.sqrt(K) / s[None]
    w8 = [pack_weight(m[:K8], "e4m3") for m in w]
    w4 = [pack_weight(m[K8:], "e2m1") for m in w]
    return {
        "xT": (n((K, T)) * s).astype(np.float32),
        "w8_words": np.stack([m[0] for m in w8]),
        "w8_scales": np.stack([m[1] for m in w8]),
        "w4_words": np.stack([m[0] for m in w4]),
        "w4_scales": np.stack([m[1] for m in w4]),
        "gate": np.stack([np.tile(r, (N, 1)) for r in g]).astype(np.float32),
        "offs": striped(slot_token),
        "pos1": striped(pos[0]),
        "pos2": striped(pos[1]),
        "pos3": striped(pos[2]),
        "pos4": striped(pos[3]),
    }


def reference(xT, w8_words, w8_scales, w4_words, w4_scales, gate, offs, pos1, pos2, pos3, pos4):
    idx = unstriped(offs)
    w = np.stack([np.concatenate([unpack_weight(w8_words[e], w8_scales[e], "e4m3"), unpack_weight(w4_words[e], w4_scales[e], "e2m1")]) for e in range(E)])
    xq = mxq(f64(xT)[:, idx], 0, "e4m3")
    y = by_expert(w, xq)
    y = np.concatenate([y, np.zeros((N, PAD))], axis=1)
    return sum(f64(gate[r]) * y[:, unstriped(p)] for r, p in enumerate((pos1, pos2, pos3, pos4)))

@@ -1,0 +1,210 @@
+from contextlib import ExitStack
+
+import concourse.mybir as mybir
+from concourse.masks import make_identity
+
+K, T, E, C, N = 1536, 768, 6, 128, 384
+TOP, PAD = 4, 64
+S = E * C
+FLOPS = 2 * K * N * S
+
+F32 = mybir.dt.float32
+BF16 = mybir.dt.bfloat16
+I32 = mybir.dt.int32
+U32 = mybir.dt.uint32
+U16 = mybir.dt.uint16
+U8 = mybir.dt.uint8
+FP8X4 = mybir.dt.float8_e4m3fn_x4
+FP4X4 = mybir.dt.float4_e2m1fn_x4
+MULT = mybir.AluOpType.mult
+ADD = mybir.AluOpType.add
+
+P = 128
+PACK = 4
+K_PASS = P * PACK
+CHUNK = 256
+CHUNKS = T // CHUNK
+BLOCKS = N // P
+PASS_ORDER = (1, 2, 0)
+TAIL = 256
+
+
+def tile_moe_ecr_lin_none_kernel(
+    tc, xT, w8_words, w8_scales, w4_words, w4_scales, gate, offs, pos1, pos2, pos3, pos4, out
+):
+    nc = tc.nc
+    with ExitStack() as ctx:
+        keep = ctx.enter_context(tc.tile_pool(name="keep", bufs=1))
+        ring = ctx.enter_context(tc.tile_pool(name="ring", bufs=6))
+        stage = ctx.enter_context(tc.tile_pool(name="stage", bufs=2))
+        psum = ctx.enter_context(tc.psum_pool(name="psum", bufs=4))
+
+        w4s = keep.tile([P, 2 * E, N], U8, name="w4s", align_bytes=64)
+        w8s = keep.tile([P, E, N], U8, name="w8s", align_bytes=64)
+        nc.vector.memset(w4s[:].bitcast(I32), 0)
+        nc.vector.memset(w8s[:].bitcast(I32), 0)
+        token_bytes = [keep.tile([P, T], U8, name="token_bytes%d" % i, align_bytes=64) for i in range(2)]
+        for t in token_bytes:
+            nc.vector.memset(t[:].bitcast(I32), 0)
+        y = [keep.tile([P, S + PAD], F32, name="y%d" % b) for b in range(BLOCKS)]
+        nc.vector.memset(y[0][:, S:], 0.0)
+        for b in range(1, BLOCKS):
+            nc.scalar.copy(y[b][:, S:], y[0][:, S:])
+
+        ident = keep.tile([P, P], F32, name="ident")
+        make_identity(nc, ident[:])
+
+        for q in range(4):
+            rows = slice(4 * q, 4 * q + 4)
+            part = slice(32 * q, 32 * q + 4)
+            nc.gpsimd.dma_start(
+                w4s[part].bitcast(I32), w4_scales[:, :, rows, :].rearrange("e a q n -> q (e a) n").bitcast(I32)
+            )
+            nc.gpsimd.dma_start(
+                w8s[part].bitcast(I32), w8_scales[:, :, rows, :].rearrange("e a q n -> q (e a) n").bitcast(I32)
+            )
+
+        raw = {}
+        offs_t = keep.tile([P, S // 16], U16, name="offs_t")
+        for a in PASS_ORDER:
+            rows = xT[a * K_PASS : (a + 1) * K_PASS, :].rearrange("(p j) t -> p j t", j=PACK)
+            for c in range(CHUNKS):
+                raw[a, c] = keep.tile([P, PACK, CHUNK], F32, name="raw%d_%d" % (a, c))
+                nc.sync.dma_start(raw[a, c][:], rows[:, :, c * CHUNK : (c + 1) * CHUNK])
+            if a == PASS_ORDER[0]:
+                nc.sync.dma_start(offs_t[:], offs)
+        w4 = []
+        w8 = []
+        for g in range(E // 2):
+            pair = slice(2 * g, 2 * g + 2)
+            w4.append(keep.tile([P, 4, 2 * N], U8, name="w4_%d" % g, align_bytes=64))
+            nc.sync.dma_start(w4[g][:].bitcast(I32), w4_words[pair].rearrange("e a p b -> p (e a) b").bitcast(I32))
+            w8.append(keep.tile([P, 2, 4 * N], U8, name="w8_%d" % g, align_bytes=64))
+            nc.sync.dma_start(w8[g][:].bitcast(I32), w8_words[pair].rearrange("e a p n r -> p (e a) (n r)").bitcast(I32))
+        pos = []
+        for r, src in enumerate((pos1, pos2, pos3, pos4)):
+            pos.append(keep.tile([P, T // 16], U16, name="pos_t%d" % r))
+            nc.sync.dma_start(pos[r][:], src)
+        gates = {}
+        for b in range(BLOCKS):
+            width = T - TAIL if b == BLOCKS - 1 else T
+            for r in range(TOP):
+                gates[b, r] = keep.tile([P, width], F32, name="gate%d_%d" % (b, r))
+                nc.sync.dma_start(gates[b, r][:], gate[r, b * P : (b + 1) * P, :width])
+        tail_gate = keep.tile([P, TOP, TAIL], F32, name="tail_gate")
+        nc.sync.dma_start(tail_gate[:], gate[:, N - P :, T - TAIL :].rearrange("r p t -> p r t"))
+
+        plane = {1: (0, 0), 2: (1, 0), 0: (1, 4)}
+        token_words = {a: keep.tile([P, T], U32, name="token_words%d" % a, align_bytes=64) for a in PASS_ORDER}
+        slot_words = {a: keep.tile([P, S], U32, name="slot_words%d" % a, align_bytes=64) for a in PASS_ORDER}
+        slot_bytes = [keep.tile([P, S], U8, name="slot_bytes%d" % i, align_bytes=64) for i in range(2)]
+
+        def quantise(a, c, on_vector):
+            grouped = keep.tile([P, CHUNK, PACK], BF16, name="grouped%d_%d" % (a, c), align_bytes=64)
+            dst = grouped[:].rearrange("p (c i) j -> p c j i", i=4)
+            src = raw[a, c][:].rearrange("p j (c i) -> p c j i", i=4)
+            if on_vector:
+                nc.vector.tensor_copy(dst, src)
+            else:
+                nc.scalar.copy(dst, src)
+            cols = slice(c * CHUNK, (c + 1) * CHUNK)
+            which, first = plane[a]
+            nc.vector.quantize_mx(
+                out=token_words[a][:, cols].bitcast(FP8X4),
+                scales=token_bytes[which][first:, cols],
+                in_=grouped[:].rearrange("p t j -> p (t j)"),
+            )
+
+        def gather(dst, window, lo, hi):
+            nc.vector.tensor_copy(dst[:, lo:hi], window[:].indirect(offs_t[:, lo // 16 : hi // 16]))
+
+        first_pass, second_pass, last_pass = PASS_ORDER
+        halves = ((0, S // 2), (S // 2, S))
+        for c in range(CHUNKS):
+            quantise(first_pass, c, c == CHUNKS - 1)
+        for lo, hi in halves:
+            gather(slot_words[first_pass], token_words[first_pass], lo, hi)
+        for lo, hi in halves:
+            gather(slot_bytes[0], token_bytes[0], lo, hi)
+        for c in range(CHUNKS):
+            quantise(second_pass, c, False)
+        for lo, hi in halves:
+            gather(slot_words[second_pass], token_words[second_pass], lo, hi)
+        for c in range(CHUNKS):
+            quantise(last_pass, c, c == CHUNKS - 1)
+        expert_runs = ((0, 3), (3, 5), (5, 6))
+        for e0, e1 in expert_runs:
+            gather(slot_words[last_pass], token_words[last_pass], e0 * C, e1 * C)
+            gather(slot_bytes[1], token_bytes[1], e0 * C, e1 * C)
+
+        def experts(b, e0, e1):
+            bank = psum.tile([P, (e1 - e0) * C], F32, name="bank")
+            ncols = slice(b * P, (b + 1) * P)
+            for e in range(e0, e1):
+                slots = slice(e * C, (e + 1) * C)
+                for i, a in enumerate(PASS_ORDER):
+                    if a == 0:
+                        lhsT = w8[e // 2][:, e % 2, 4 * b * P : 4 * (b + 1) * P].bitcast(FP8X4)
+                        lhsT_scale = w8s[:, e, ncols]
+                    else:
+                        lhsT = w4[e // 2][:, 2 * (e % 2) + a - 1, 2 * b * P : 2 * (b + 1) * P].bitcast(FP4X4)
+                        lhsT_scale = w4s[:, 2 * e + a - 1, ncols]
+                    which, first = plane[a]
+                    nc.tensor.matmul_mx(
+                        out=bank[:, (e - e0) * C : (e - e0 + 1) * C],
+                        lhsT=lhsT,
+                        lhsT_scale=lhsT_scale,
+                        rhs=slot_words[a][:, slots].bitcast(FP8X4),
+                        rhs_scale=slot_bytes[which][first:, slots],
+                        start=(i == 0),
+                        stop=(i == len(PASS_ORDER) - 1),
+                    )
+            nc.scalar.copy(y[b][:, e0 * C : e1 * C], bank[:])
+
+        for e0, e1 in expert_runs:
+            experts(0, e0, e1)
+        for b in range(1, BLOCKS):
+            for e0, e1 in ((0, 3), (3, 6)):
+                experts(b, e0, e1)
+
+        def product(b, r, lo, hi, g):
+            prod = ring.tile([P, hi - lo], F32, name="prod")
+            nc.vector.tensor_tensor(prod[:], y[b][:].indirect(pos[r][:, lo // 16 : hi // 16]), g, MULT)
+            return prod
+
+        for b in range(BLOCKS):
+            width = T - TAIL if b == BLOCKS - 1 else T
+            half = width // 2
+            per_bank = half // P
+            turned = [psum.tile([P, half], F32, name="turned") for h in range(2)]
+            for r in range(TOP):
+                prod = product(b, r, 0, width, gates[b, r][:])
+                for h in range(2):
+                    for j in range(per_bank):
+                        t0 = h * half + j * P
+                        nc.tensor.matmul(
+                            turned[h][:, j * P : (j + 1) * P],
+                            lhsT=prod[:, t0 : t0 + P],
+                            rhs=ident[:],
+                            start=(r == 0 and j == 0),
+                            stop=(r == TOP - 1 and j == per_bank - 1),
+                            is_transpose=True,
+                        )
+            result = stage.tile([P, width], F32, name="result")
+            for h in range(2):
+                sums = stage.tile([P, half], F32, name="sums")
+                nc.scalar.copy(sums[:], turned[h][:])
+                bank = psum.tile([P, half], F32, name="bank")
+                for j in range(per_bank):
+                    nc.tensor.transpose(bank[:, j * P : (j + 1) * P], sums[:, j * P : (j + 1) * P], ident[:])
+                nc.scalar.copy(result[:, h * half : (h + 1) * half], bank[:])
+            nc.scalar.dma_start(out[b * P : (b + 1) * P, :width], result[:])
+
+        b = BLOCKS - 1
+        prods = [product(b, r, T - TAIL, T, tail_gate[:, r, :]) for r in range(TOP - 1)]
+        acc = [keep.tile([P, TAIL], F32, name="acc%d" % i) for i in range(TOP - 1)]
+        nc.vector.tensor_tensor(acc[0][:], prods[0][:], prods[1][:], ADD)
+        prods.append(product(b, TOP - 1, T - TAIL, T, tail_gate[:, TOP - 1, :]))
+        nc.vector.tensor_tensor(acc[1][:], acc[0][:], prods[2][:], ADD)
+        nc.vector.tensor_tensor(acc[2][:], acc[1][:], prods[3][:], ADD)
+        nc.sync.dma_start(out[N - P :, T - TAIL :], acc[2][:])

@@ -22,11 +22,10 @@ ADD = mybir.AluOpType.add
 P = 128
 PACK = 4
 K_PASS = P * PACK
-CHUNK = 256
-CHUNKS = T // CHUNK
+CHUNKS = ((0, 512), (512, T))
 BLOCKS = N // P
 PASS_ORDER = (1, 2, 0)
-TAIL = 256
+TURNED_LAST = 256
 
 
 def tile_moe_ecr_lin_none_kernel(
@@ -35,14 +34,12 @@ def tile_moe_ecr_lin_none_kernel(
     nc = tc.nc
     with ExitStack() as ctx:
         keep = ctx.enter_context(tc.tile_pool(name="keep", bufs=1))
-        ring = ctx.enter_context(tc.tile_pool(name="ring", bufs=6))
+        ring = ctx.enter_context(tc.tile_pool(name="ring", bufs=8))
         stage = ctx.enter_context(tc.tile_pool(name="stage", bufs=2))
         psum = ctx.enter_context(tc.psum_pool(name="psum", bufs=4))
 
-        w4s = keep.tile([P, 2 * E, N], U8, name="w4s", align_bytes=64)
-        w8s = keep.tile([P, E, N], U8, name="w8s", align_bytes=64)
-        nc.vector.memset(w4s[:].bitcast(I32), 0)
-        nc.vector.memset(w8s[:].bitcast(I32), 0)
+        w_bytes = keep.tile([P, 2 * E, N], U8, name="w_bytes", align_bytes=64)
+        nc.vector.memset(w_bytes[:].bitcast(I32), 0)
         token_bytes = [keep.tile([P, T], U8, name="token_bytes%d" % i, align_bytes=64) for i in range(2)]
         for t in token_bytes:
             nc.vector.memset(t[:].bitcast(I32), 0)
@@ -54,23 +51,21 @@ def tile_moe_ecr_lin_none_kernel(
         ident = keep.tile([P, P], F32, name="ident")
         make_identity(nc, ident[:])
 
-        for q in range(4):
-            rows = slice(4 * q, 4 * q + 4)
-            part = slice(32 * q, 32 * q + 4)
-            nc.gpsimd.dma_start(
-                w4s[part].bitcast(I32), w4_scales[:, :, rows, :].rearrange("e a q n -> q (e a) n").bitcast(I32)
-            )
-            nc.gpsimd.dma_start(
-                w8s[part].bitcast(I32), w8_scales[:, :, rows, :].rearrange("e a q n -> q (e a) n").bitcast(I32)
-            )
+        for queue, source, first, rows in ((nc.gpsimd, w4_scales, 0, 2 * E), (nc.scalar, w8_scales, 4, E)):
+            for q in range(4):
+                queue.dma_start(
+                    w_bytes[32 * q + first : 32 * q + first + 4, :rows, :].bitcast(I32),
+                    source[:, :, 4 * q : 4 * q + 4, :].rearrange("e a q n -> q (e a) n").bitcast(I32),
+                )
 
+        last = BLOCKS - 1
         raw = {}
         offs_t = keep.tile([P, S // 16], U16, name="offs_t")
         for a in PASS_ORDER:
             rows = xT[a * K_PASS : (a + 1) * K_PASS, :].rearrange("(p j) t -> p j t", j=PACK)
-            for c in range(CHUNKS):
-                raw[a, c] = keep.tile([P, PACK, CHUNK], F32, name="raw%d_%d" % (a, c))
-                nc.sync.dma_start(raw[a, c][:], rows[:, :, c * CHUNK : (c + 1) * CHUNK])
+            for lo, hi in CHUNKS:
+                raw[a, lo] = keep.tile([P, PACK, hi - lo], F32, name="raw%d_%d" % (a, lo))
+                nc.sync.dma_start(raw[a, lo][:], rows[:, :, lo:hi])
             if a == PASS_ORDER[0]:
                 nc.sync.dma_start(offs_t[:], offs)
         w4 = []
@@ -82,73 +77,74 @@ def tile_moe_ecr_lin_none_kernel(
             w8.append(keep.tile([P, 2, 4 * N], U8, name="w8_%d" % g, align_bytes=64))
             nc.sync.dma_start(w8[g][:].bitcast(I32), w8_words[pair].rearrange("e a p n r -> p (e a) (n r)").bitcast(I32))
         pos = []
-        for r, src in enumerate((pos1, pos2, pos3, pos4)):
-            pos.append(keep.tile([P, T // 16], U16, name="pos_t%d" % r))
-            nc.sync.dma_start(pos[r][:], src)
         gates = {}
-        for b in range(BLOCKS):
-            width = T - TAIL if b == BLOCKS - 1 else T
-            for r in range(TOP):
-                gates[b, r] = keep.tile([P, width], F32, name="gate%d_%d" % (b, r))
-                nc.sync.dma_start(gates[b, r][:], gate[r, b * P : (b + 1) * P, :width])
-        tail_gate = keep.tile([P, TOP, TAIL], F32, name="tail_gate")
-        nc.sync.dma_start(tail_gate[:], gate[:, N - P :, T - TAIL :].rearrange("r p t -> p r t"))
+        for b in range(last):
+            for r, source in enumerate((pos1, pos2, pos3, pos4)):
+                gates[b, r] = keep.tile([P, T], F32, name="gate%d_%d" % (b, r))
+                nc.sync.dma_start(gates[b, r][:], gate[r, b * P : (b + 1) * P, :])
+                if b == 0:
+                    pos.append(keep.tile([P, T // 16], U16, name="pos_t%d" % r))
+                    nc.sync.dma_start(pos[r][:], source)
+        gate_head = keep.tile([P, TOP, TURNED_LAST], F32, name="gate_head")
+        nc.sync.dma_start(gate_head[:], gate[:, last * P :, :TURNED_LAST].rearrange("r p t -> p r t"))
+        gate_tail = []
+        for r in range(TOP):
+            gates[last, r] = gate_head[:, r, :]
+            gate_tail.append(keep.tile([P, T - TURNED_LAST], F32, name="gate_tail%d" % r))
+            nc.sync.dma_start(gate_tail[r][:], gate[r, last * P :, TURNED_LAST:])
 
         plane = {1: (0, 0), 2: (1, 0), 0: (1, 4)}
         token_words = {a: keep.tile([P, T], U32, name="token_words%d" % a, align_bytes=64) for a in PASS_ORDER}
         slot_words = {a: keep.tile([P, S], U32, name="slot_words%d" % a, align_bytes=64) for a in PASS_ORDER}
         slot_bytes = [keep.tile([P, S], U8, name="slot_bytes%d" % i, align_bytes=64) for i in range(2)]
 
-        def quantise(a, c, on_vector):
-            grouped = keep.tile([P, CHUNK, PACK], BF16, name="grouped%d_%d" % (a, c), align_bytes=64)
-            dst = grouped[:].rearrange("p (c i) j -> p c j i", i=4)
-            src = raw[a, c][:].rearrange("p j (c i) -> p c j i", i=4)
-            if on_vector:
-                nc.vector.tensor_copy(dst, src)
-            else:
-                nc.scalar.copy(dst, src)
-            cols = slice(c * CHUNK, (c + 1) * CHUNK)
+        def quantise(a, engines):
+            grouped = {}
+            for (lo, hi), copy in zip(CHUNKS, engines):
+                grouped[lo] = keep.tile([P, hi - lo, PACK], BF16, name="grouped%d_%d" % (a, lo), align_bytes=64)
+                copy(
+                    grouped[lo][:].rearrange("p (c i) j -> p c j i", i=4),
+                    raw[a, lo][:].rearrange("p j (c i) -> p c j i", i=4),
+                )
             which, first = plane[a]
-            nc.vector.quantize_mx(
-                out=token_words[a][:, cols].bitcast(FP8X4),
-                scales=token_bytes[which][first:, cols],
-                in_=grouped[:].rearrange("p t j -> p (t j)"),
-            )
+            for lo, hi in CHUNKS:
+                nc.vector.quantize_mx(
+                    out=token_words[a][:, lo:hi].bitcast(FP8X4),
+                    scales=token_bytes[which][first:, lo:hi],
+                    in_=grouped[lo][:].rearrange("p t j -> p (t j)"),
+                )
 
         def gather(dst, window, lo, hi):
             nc.vector.tensor_copy(dst[:, lo:hi], window[:].indirect(offs_t[:, lo // 16 : hi // 16]))
 
         first_pass, second_pass, last_pass = PASS_ORDER
         halves = ((0, S // 2), (S // 2, S))
-        for c in range(CHUNKS):
-            quantise(first_pass, c, c == CHUNKS - 1)
+        on_vector, on_scalar = nc.vector.tensor_copy, nc.scalar.copy
+        quantise(first_pass, (on_vector, on_scalar))
         for lo, hi in halves:
             gather(slot_words[first_pass], token_words[first_pass], lo, hi)
         for lo, hi in halves:
             gather(slot_bytes[0], token_bytes[0], lo, hi)
-        for c in range(CHUNKS):
-            quantise(second_pass, c, False)
+        quantise(second_pass, (on_scalar, on_scalar))
         for lo, hi in halves:
             gather(slot_words[second_pass], token_words[second_pass], lo, hi)
-        for c in range(CHUNKS):
-            quantise(last_pass, c, c == CHUNKS - 1)
-        expert_runs = ((0, 3), (3, 5), (5, 6))
+        quantise(last_pass, (on_scalar, on_vector))
+        expert_runs = tuple((e, e + 2) for e in range(0, E, 2))
         for e0, e1 in expert_runs:
             gather(slot_words[last_pass], token_words[last_pass], e0 * C, e1 * C)
             gather(slot_bytes[1], token_bytes[1], e0 * C, e1 * C)
 
         def experts(b, e0, e1):
             bank = psum.tile([P, (e1 - e0) * C], F32, name="bank")
-            ncols = slice(b * P, (b + 1) * P)
             for e in range(e0, e1):
                 slots = slice(e * C, (e + 1) * C)
                 for i, a in enumerate(PASS_ORDER):
                     if a == 0:
                         lhsT = w8[e // 2][:, e % 2, 4 * b * P : 4 * (b + 1) * P].bitcast(FP8X4)
-                        lhsT_scale = w8s[:, e, ncols]
+                        lhsT_scale = w_bytes[4:, e, b * P : (b + 1) * P]
                     else:
                         lhsT = w4[e // 2][:, 2 * (e % 2) + a - 1, 2 * b * P : 2 * (b + 1) * P].bitcast(FP4X4)
-                        lhsT_scale = w4s[:, 2 * e + a - 1, ncols]
+                        lhsT_scale = w_bytes[:, 2 * e + a - 1, b * P : (b + 1) * P]
                     which, first = plane[a]
                     nc.tensor.matmul_mx(
                         out=bank[:, (e - e0) * C : (e - e0 + 1) * C],
@@ -161,27 +157,26 @@ def tile_moe_ecr_lin_none_kernel(
                     )
             nc.scalar.copy(y[b][:, e0 * C : e1 * C], bank[:])
 
-        for e0, e1 in expert_runs:
-            experts(0, e0, e1)
-        for b in range(1, BLOCKS):
-            for e0, e1 in ((0, 3), (3, 6)):
+        for b in range(BLOCKS):
+            for e0, e1 in expert_runs:
                 experts(b, e0, e1)
 
         def product(b, r, lo, hi, g):
             prod = ring.tile([P, hi - lo], F32, name="prod")
-            nc.vector.tensor_tensor(prod[:], y[b][:].indirect(pos[r][:, lo // 16 : hi // 16]), g, MULT)
+            nc.vector.tensor_tensor(prod[:], y[b][:].indirect(pos[r][:, lo // 16 : hi // 16]), g[:], MULT)
             return prod
 
         for b in range(BLOCKS):
-            width = T - TAIL if b == BLOCKS - 1 else T
-            half = width // 2
-            per_bank = half // P
-            turned = [psum.tile([P, half], F32, name="turned") for h in range(2)]
+            width = TURNED_LAST if b == last else T
+            banks = 1 if b == last else 2
+            part = width // banks
+            per_bank = part // P
+            turned = [psum.tile([P, part], F32, name="turned") for h in range(banks)]
             for r in range(TOP):
-                prod = product(b, r, 0, width, gates[b, r][:])
-                for h in range(2):
+                prod = product(b, r, 0, width, gates[b, r])
+                for h in range(banks):
                     for j in range(per_bank):
-                        t0 = h * half + j * P
+                        t0 = h * part + j * P
                         nc.tensor.matmul(
                             turned[h][:, j * P : (j + 1) * P],
                             lhsT=prod[:, t0 : t0 + P],
@@ -191,20 +186,21 @@ def tile_moe_ecr_lin_none_kernel(
                             is_transpose=True,
                         )
             result = stage.tile([P, width], F32, name="result")
-            for h in range(2):
-                sums = stage.tile([P, half], F32, name="sums")
+            for h in range(banks):
+                sums = stage.tile([P, part], F32, name="sums")
                 nc.scalar.copy(sums[:], turned[h][:])
-                bank = psum.tile([P, half], F32, name="bank")
+                bank = psum.tile([P, part], F32, name="bank")
                 for j in range(per_bank):
                     nc.tensor.transpose(bank[:, j * P : (j + 1) * P], sums[:, j * P : (j + 1) * P], ident[:])
-                nc.scalar.copy(result[:, h * half : (h + 1) * half], bank[:])
+                nc.scalar.copy(result[:, h * part : (h + 1) * part], bank[:])
             nc.scalar.dma_start(out[b * P : (b + 1) * P, :width], result[:])
 
-        b = BLOCKS - 1
-        prods = [product(b, r, T - TAIL, T, tail_gate[:, r, :]) for r in range(TOP - 1)]
-        acc = [keep.tile([P, TAIL], F32, name="acc%d" % i) for i in range(TOP - 1)]
+        rest = T - TURNED_LAST
+        prods = [product(last, r, TURNED_LAST, T, gate_tail[r]) for r in range(TOP - 1)]
+        acc = [keep.tile([P, rest], F32, name="acc%d" % i) for i in range(TOP - 1)]
         nc.vector.tensor_tensor(acc[0][:], prods[0][:], prods[1][:], ADD)
-        prods.append(product(b, TOP - 1, T - TAIL, T, tail_gate[:, TOP - 1, :]))
+        prods.append(product(last, TOP - 1, TURNED_LAST, T, gate_tail[TOP - 1]))
         nc.vector.tensor_tensor(acc[1][:], acc[0][:], prods[2][:], ADD)
-        nc.vector.tensor_tensor(acc[2][:], acc[1][:], prods[3][:], ADD)
-        nc.sync.dma_start(out[N - P :, T - TAIL :], acc[2][:])
+        for lo, hi in ((0, rest // 2), (rest // 2, rest)):
+            nc.vector.tensor_tensor(acc[2][:, lo:hi], acc[1][:, lo:hi], prods[3][:, lo:hi], ADD)
+            nc.sync.dma_start(out[last * P :, TURNED_LAST + lo : TURNED_LAST + hi], acc[2][:, lo:hi])

@@ -43,7 +43,7 @@ def tile_moe_ecr_lin_none_kernel(
         token_bytes = [keep.tile([P, T], U8, name="token_bytes%d" % i, align_bytes=64) for i in range(2)]
         for t in token_bytes:
             nc.vector.memset(t[:].bitcast(I32), 0)
-        y = [keep.tile([P, S + PAD], F32, name="y%d" % b) for b in range(BLOCKS)]
+        y = [keep.tile([P, S + PAD], F32, name="y%d" % b, align_bytes=64) for b in range(BLOCKS)]
         nc.vector.memset(y[0][:, S:], 0.0)
         for b in range(1, BLOCKS):
             nc.scalar.copy(y[b][:, S:], y[0][:, S:])
@@ -63,11 +63,16 @@ def tile_moe_ecr_lin_none_kernel(
         offs_t = keep.tile([P, S // 16], U16, name="offs_t")
         for a in PASS_ORDER:
             rows = xT[a * K_PASS : (a + 1) * K_PASS, :].rearrange("(p j) t -> p j t", j=PACK)
-            for lo, hi in CHUNKS:
-                raw[a, lo] = keep.tile([P, PACK, hi - lo], F32, name="raw%d_%d" % (a, lo))
-                nc.sync.dma_start(raw[a, lo][:], rows[:, :, lo:hi])
             if a == PASS_ORDER[0]:
+                whole = keep.tile([P, PACK, T], F32, name="raw%d" % a)
+                nc.sync.dma_start(whole[:], rows)
                 nc.sync.dma_start(offs_t[:], offs)
+                for lo, hi in CHUNKS:
+                    raw[a, lo] = whole[:, :, lo:hi]
+            else:
+                for lo, hi in CHUNKS:
+                    raw[a, lo] = keep.tile([P, PACK, hi - lo], F32, name="raw%d_%d" % (a, lo))
+                    nc.sync.dma_start(raw[a, lo][:], rows[:, :, lo:hi])
         w4 = []
         w8 = []
         for g in range(E // 2):
@@ -131,33 +136,46 @@ def tile_moe_ecr_lin_none_kernel(
         quantise(last_pass, (on_scalar, on_vector))
         expert_runs = tuple((e, e + 2) for e in range(0, E, 2))
         for e0, e1 in expert_runs:
-            gather(slot_words[last_pass], token_words[last_pass], e0 * C, e1 * C)
             gather(slot_bytes[1], token_bytes[1], e0 * C, e1 * C)
+            gather(slot_words[last_pass], token_words[last_pass], e0 * C, e1 * C)
+
+        def one_pass(dst, b, e, a):
+            slots = slice(e * C, (e + 1) * C)
+            if a == 0:
+                lhsT = w8[e // 2][:, e % 2, 4 * b * P : 4 * (b + 1) * P].bitcast(FP8X4)
+                lhsT_scale = w_bytes[4:, e, b * P : (b + 1) * P]
+            else:
+                lhsT = w4[e // 2][:, 2 * (e % 2) + a - 1, 2 * b * P : 2 * (b + 1) * P].bitcast(FP4X4)
+                lhsT_scale = w_bytes[:, 2 * e + a - 1, b * P : (b + 1) * P]
+            which, first = plane[a]
+            nc.tensor.matmul_mx(
+                out=dst,
+                lhsT=lhsT,
+                lhsT_scale=lhsT_scale,
+                rhs=slot_words[a][:, slots].bitcast(FP8X4),
+                rhs_scale=slot_bytes[which][first:, slots],
+                start=(a == first_pass),
+                stop=(a == last_pass),
+            )
 
         def experts(b, e0, e1):
             bank = psum.tile([P, (e1 - e0) * C], F32, name="bank")
             for e in range(e0, e1):
-                slots = slice(e * C, (e + 1) * C)
-                for i, a in enumerate(PASS_ORDER):
-                    if a == 0:
-                        lhsT = w8[e // 2][:, e % 2, 4 * b * P : 4 * (b + 1) * P].bitcast(FP8X4)
-                        lhsT_scale = w_bytes[4:, e, b * P : (b + 1) * P]
-                    else:
-                        lhsT = w4[e // 2][:, 2 * (e % 2) + a - 1, 2 * b * P : 2 * (b + 1) * P].bitcast(FP4X4)
-                        lhsT_scale = w_bytes[:, 2 * e + a - 1, b * P : (b + 1) * P]
-                    which, first = plane[a]
-                    nc.tensor.matmul_mx(
-                        out=bank[:, (e - e0) * C : (e - e0 + 1) * C],
-                        lhsT=lhsT,
-                        lhsT_scale=lhsT_scale,
-                        rhs=slot_words[a][:, slots].bitcast(FP8X4),
-                        rhs_scale=slot_bytes[which][first:, slots],
-                        start=(i == 0),
-                        stop=(i == len(PASS_ORDER) - 1),
-                    )
+                for a in PASS_ORDER:
+                    one_pass(bank[:, (e - e0) * C : (e - e0 + 1) * C], b, e, a)
             nc.scalar.copy(y[b][:, e0 * C : e1 * C], bank[:])
 
-        for b in range(BLOCKS):
+        for e0, e1 in expert_runs[:-1]:
+            experts(0, e0, e1)
+        closing = range(*expert_runs[-1])
+        own_bank = {e: psum.tile([P, C], F32, name="bank") for e in closing}
+        for e in closing:
+            for a in (first_pass, second_pass):
+                one_pass(own_bank[e][:], 0, e, a)
+        for e in closing:
+            one_pass(own_bank[e][:], 0, e, last_pass)
+            nc.scalar.copy(y[0][:, e * C : (e + 1) * C], own_bank[e][:])
+        for b in range(1, BLOCKS):
             for e0, e1 in expert_runs:
                 experts(b, e0, e1)
 
@@ -200,7 +218,9 @@ def tile_moe_ecr_lin_none_kernel(
         acc = [keep.tile([P, rest], F32, name="acc%d" % i) for i in range(TOP - 1)]
         nc.vector.tensor_tensor(acc[0][:], prods[0][:], prods[1][:], ADD)
         prods.append(product(last, TOP - 1, TURNED_LAST, T, gate_tail[TOP - 1]))
-        nc.vector.tensor_tensor(acc[1][:], acc[0][:], prods[2][:], ADD)
-        for lo, hi in ((0, rest // 2), (rest // 2, rest)):
+        pieces = ((0, rest // 2), (rest // 2, rest))
+        for lo, hi in pieces:
+            nc.vector.tensor_tensor(acc[1][:, lo:hi], acc[0][:, lo:hi], prods[2][:, lo:hi], ADD)
+        for lo, hi in pieces:
             nc.vector.tensor_tensor(acc[2][:, lo:hi], acc[1][:, lo:hi], prods[3][:, lo:hi], ADD)
             nc.sync.dma_start(out[last * P :, TURNED_LAST + lo : TURNED_LAST + hi], acc[2][:, lo:hi])

from contextlib import ExitStack

import concourse.mybir as mybir
from concourse.masks import make_identity

K, T, E, C, N = 1536, 768, 6, 128, 384
TOP, PAD = 4, 64
S = E * C
FLOPS = 2 * K * N * S

F32 = mybir.dt.float32
BF16 = mybir.dt.bfloat16
I32 = mybir.dt.int32
U32 = mybir.dt.uint32
U16 = mybir.dt.uint16
U8 = mybir.dt.uint8
FP8X4 = mybir.dt.float8_e4m3fn_x4
FP4X4 = mybir.dt.float4_e2m1fn_x4
MULT = mybir.AluOpType.mult
ADD = mybir.AluOpType.add

P = 128
PACK = 4
K_PASS = P * PACK
CHUNKS = ((0, 512), (512, T))
BLOCKS = N // P
PASS_ORDER = (1, 2, 0)
TURNED_LAST = 256


def tile_moe_ecr_lin_none_kernel(
    tc, xT, w8_words, w8_scales, w4_words, w4_scales, gate, offs, pos1, pos2, pos3, pos4, out
):
    nc = tc.nc
    with ExitStack() as ctx:
        keep = ctx.enter_context(tc.tile_pool(name="keep", bufs=1))
        ring = ctx.enter_context(tc.tile_pool(name="ring", bufs=8))
        stage = ctx.enter_context(tc.tile_pool(name="stage", bufs=2))
        psum = ctx.enter_context(tc.psum_pool(name="psum", bufs=4))

        w_bytes = keep.tile([P, 2 * E, N], U8, name="w_bytes", align_bytes=64)
        nc.vector.memset(w_bytes[:].bitcast(I32), 0)
        token_bytes = [keep.tile([P, T], U8, name="token_bytes%d" % i, align_bytes=64) for i in range(2)]
        for t in token_bytes:
            nc.vector.memset(t[:].bitcast(I32), 0)
        y = [keep.tile([P, S + PAD], F32, name="y%d" % b, align_bytes=64) for b in range(BLOCKS)]
        nc.vector.memset(y[0][:, S:], 0.0)
        for b in range(1, BLOCKS):
            nc.scalar.copy(y[b][:, S:], y[0][:, S:])

        ident = keep.tile([P, P], F32, name="ident")
        make_identity(nc, ident[:])

        for queue, source, first, rows in ((nc.gpsimd, w4_scales, 0, 2 * E), (nc.scalar, w8_scales, 4, E)):
            for q in range(4):
                queue.dma_start(
                    w_bytes[32 * q + first : 32 * q + first + 4, :rows, :].bitcast(I32),
                    source[:, :, 4 * q : 4 * q + 4, :].rearrange("e a q n -> q (e a) n").bitcast(I32),
                )

        last = BLOCKS - 1
        raw = {}
        offs_t = keep.tile([P, S // 16], U16, name="offs_t")
        for a in PASS_ORDER:
            rows = xT[a * K_PASS : (a + 1) * K_PASS, :].rearrange("(p j) t -> p j t", j=PACK)
            if a == PASS_ORDER[0]:
                whole = keep.tile([P, PACK, T], F32, name="raw%d" % a)
                nc.sync.dma_start(whole[:], rows)
                nc.sync.dma_start(offs_t[:], offs)
                for lo, hi in CHUNKS:
                    raw[a, lo] = whole[:, :, lo:hi]
            else:
                for lo, hi in CHUNKS:
                    raw[a, lo] = keep.tile([P, PACK, hi - lo], F32, name="raw%d_%d" % (a, lo))
                    nc.sync.dma_start(raw[a, lo][:], rows[:, :, lo:hi])
        w4 = []
        w8 = []
        for g in range(E // 2):
            pair = slice(2 * g, 2 * g + 2)
            w4.append(keep.tile([P, 4, 2 * N], U8, name="w4_%d" % g, align_bytes=64))
            nc.sync.dma_start(w4[g][:].bitcast(I32), w4_words[pair].rearrange("e a p b -> p (e a) b").bitcast(I32))
            w8.append(keep.tile([P, 2, 4 * N], U8, name="w8_%d" % g, align_bytes=64))
            nc.sync.dma_start(w8[g][:].bitcast(I32), w8_words[pair].rearrange("e a p n r -> p (e a) (n r)").bitcast(I32))
        pos = []
        gates = {}
        for b in range(last):
            for r, source in enumerate((pos1, pos2, pos3, pos4)):
                gates[b, r] = keep.tile([P, T], F32, name="gate%d_%d" % (b, r))
                nc.sync.dma_start(gates[b, r][:], gate[r, b * P : (b + 1) * P, :])
                if b == 0:
                    pos.append(keep.tile([P, T // 16], U16, name="pos_t%d" % r))
                    nc.sync.dma_start(pos[r][:], source)
        gate_head = keep.tile([P, TOP, TURNED_LAST], F32, name="gate_head")
        nc.sync.dma_start(gate_head[:], gate[:, last * P :, :TURNED_LAST].rearrange("r p t -> p r t"))
        gate_tail = []
        for r in range(TOP):
            gates[last, r] = gate_head[:, r, :]
            gate_tail.append(keep.tile([P, T - TURNED_LAST], F32, name="gate_tail%d" % r))
            nc.sync.dma_start(gate_tail[r][:], gate[r, last * P :, TURNED_LAST:])

        plane = {1: (0, 0), 2: (1, 0), 0: (1, 4)}
        token_words = {a: keep.tile([P, T], U32, name="token_words%d" % a, align_bytes=64) for a in PASS_ORDER}
        slot_words = {a: keep.tile([P, S], U32, name="slot_words%d" % a, align_bytes=64) for a in PASS_ORDER}
        slot_bytes = [keep.tile([P, S], U8, name="slot_bytes%d" % i, align_bytes=64) for i in range(2)]

        def quantise(a, engines):
            grouped = {}
            for (lo, hi), copy in zip(CHUNKS, engines):
                grouped[lo] = keep.tile([P, hi - lo, PACK], BF16, name="grouped%d_%d" % (a, lo), align_bytes=64)
                copy(
                    grouped[lo][:].rearrange("p (c i) j -> p c j i", i=4),
                    raw[a, lo][:].rearrange("p j (c i) -> p c j i", i=4),
                )
            which, first = plane[a]
            for lo, hi in CHUNKS:
                nc.vector.quantize_mx(
                    out=token_words[a][:, lo:hi].bitcast(FP8X4),
                    scales=token_bytes[which][first:, lo:hi],
                    in_=grouped[lo][:].rearrange("p t j -> p (t j)"),
                )

        def gather(dst, window, lo, hi):
            nc.vector.tensor_copy(dst[:, lo:hi], window[:].indirect(offs_t[:, lo // 16 : hi // 16]))

        first_pass, second_pass, last_pass = PASS_ORDER
        halves = ((0, S // 2), (S // 2, S))
        on_vector, on_scalar = nc.vector.tensor_copy, nc.scalar.copy
        quantise(first_pass, (on_vector, on_scalar))
        for lo, hi in halves:
            gather(slot_words[first_pass], token_words[first_pass], lo, hi)
        for lo, hi in halves:
            gather(slot_bytes[0], token_bytes[0], lo, hi)
        quantise(second_pass, (on_scalar, on_scalar))
        for lo, hi in halves:
            gather(slot_words[second_pass], token_words[second_pass], lo, hi)
        quantise(last_pass, (on_scalar, on_vector))
        expert_runs = tuple((e, e + 2) for e in range(0, E, 2))
        for e0, e1 in expert_runs:
            gather(slot_bytes[1], token_bytes[1], e0 * C, e1 * C)
            gather(slot_words[last_pass], token_words[last_pass], e0 * C, e1 * C)

        def one_pass(dst, b, e, a):
            slots = slice(e * C, (e + 1) * C)
            if a == 0:
                lhsT = w8[e // 2][:, e % 2, 4 * b * P : 4 * (b + 1) * P].bitcast(FP8X4)
                lhsT_scale = w_bytes[4:, e, b * P : (b + 1) * P]
            else:
                lhsT = w4[e // 2][:, 2 * (e % 2) + a - 1, 2 * b * P : 2 * (b + 1) * P].bitcast(FP4X4)
                lhsT_scale = w_bytes[:, 2 * e + a - 1, b * P : (b + 1) * P]
            which, first = plane[a]
            nc.tensor.matmul_mx(
                out=dst,
                lhsT=lhsT,
                lhsT_scale=lhsT_scale,
                rhs=slot_words[a][:, slots].bitcast(FP8X4),
                rhs_scale=slot_bytes[which][first:, slots],
                start=(a == first_pass),
                stop=(a == last_pass),
            )

        def experts(b, e0, e1):
            bank = psum.tile([P, (e1 - e0) * C], F32, name="bank")
            for e in range(e0, e1):
                for a in PASS_ORDER:
                    one_pass(bank[:, (e - e0) * C : (e - e0 + 1) * C], b, e, a)
            nc.scalar.copy(y[b][:, e0 * C : e1 * C], bank[:])

        for e0, e1 in expert_runs[:-1]:
            experts(0, e0, e1)
        closing = range(*expert_runs[-1])
        own_bank = {e: psum.tile([P, C], F32, name="bank") for e in closing}
        for e in closing:
            for a in (first_pass, second_pass):
                one_pass(own_bank[e][:], 0, e, a)
        for e in closing:
            one_pass(own_bank[e][:], 0, e, last_pass)
            nc.scalar.copy(y[0][:, e * C : (e + 1) * C], own_bank[e][:])
        for b in range(1, BLOCKS):
            for e0, e1 in expert_runs:
                experts(b, e0, e1)

        def product(b, r, lo, hi, g):
            prod = ring.tile([P, hi - lo], F32, name="prod")
            nc.vector.tensor_tensor(prod[:], y[b][:].indirect(pos[r][:, lo // 16 : hi // 16]), g[:], MULT)
            return prod

        for b in range(BLOCKS):
            width = TURNED_LAST if b == last else T
            banks = 1 if b == last else 2
            part = width // banks
            per_bank = part // P
            turned = [psum.tile([P, part], F32, name="turned") for h in range(banks)]
            for r in range(TOP):
                prod = product(b, r, 0, width, gates[b, r])
                for h in range(banks):
                    for j in range(per_bank):
                        t0 = h * part + j * P
                        nc.tensor.matmul(
                            turned[h][:, j * P : (j + 1) * P],
                            lhsT=prod[:, t0 : t0 + P],
                            rhs=ident[:],
                            start=(r == 0 and j == 0),
                            stop=(r == TOP - 1 and j == per_bank - 1),
                            is_transpose=True,
                        )
            result = stage.tile([P, width], F32, name="result")
            for h in range(banks):
                sums = stage.tile([P, part], F32, name="sums")
                nc.scalar.copy(sums[:], turned[h][:])
                bank = psum.tile([P, part], F32, name="bank")
                for j in range(per_bank):
                    nc.tensor.transpose(bank[:, j * P : (j + 1) * P], sums[:, j * P : (j + 1) * P], ident[:])
                nc.scalar.copy(result[:, h * part : (h + 1) * part], bank[:])
            nc.scalar.dma_start(out[b * P : (b + 1) * P, :width], result[:])

        rest = T - TURNED_LAST
        prods = [product(last, r, TURNED_LAST, T, gate_tail[r]) for r in range(TOP - 1)]
        acc = [keep.tile([P, rest], F32, name="acc%d" % i) for i in range(TOP - 1)]
        nc.vector.tensor_tensor(acc[0][:], prods[0][:], prods[1][:], ADD)
        prods.append(product(last, TOP - 1, TURNED_LAST, T, gate_tail[TOP - 1]))
        pieces = ((0, rest // 2), (rest // 2, rest))
        for lo, hi in pieces:
            nc.vector.tensor_tensor(acc[1][:, lo:hi], acc[0][:, lo:hi], prods[2][:, lo:hi], ADD)
        for lo, hi in pieces:
            nc.vector.tensor_tensor(acc[2][:, lo:hi], acc[1][:, lo:hi], prods[3][:, lo:hi], ADD)
            nc.sync.dma_start(out[last * P :, TURNED_LAST + lo : TURNED_LAST + hi], acc[2][:, lo:hi])
